import numpy as np
import ml_dtypes


def mxq(x, axis, fmt="e4m3"):
    dtype, down = {"e4m3": (ml_dtypes.float8_e4m3fn, 7), "e5m2": (ml_dtypes.float8_e5m2, 14)}[fmt]
    v = np.moveaxis(np.asarray(x, np.float32).astype(ml_dtypes.bfloat16).astype(np.float64), axis, -1)
    blocks = v.reshape(v.shape[:-1] + (-1, 32))
    amax = np.abs(blocks).max(-1, keepdims=True)
    byte = np.maximum(np.where(amax > 0, np.frexp(amax)[1] - 1 + 127, 0) - down, 1)
    scale = np.exp2(byte - 127.0)
    codes = (blocks / scale).astype(np.float32).astype(dtype).astype(np.float64)
    return np.moveaxis((codes * scale).reshape(v.shape), -1, axis)


WIDE = False


def mx_kscale(k):
    if not WIDE:
        return np.ones(k)
    levels = np.array([10, -10, 5, -5, 0])
    if k % 512:
        return np.exp2(np.random.permutation(np.resize(levels, k // 32))).repeat(32)
    a = np.empty((k // 512, 16))
    for p in range(k // 512):
        a[p, :8] = np.random.permutation(np.resize(levels, 8))
        for g in range(8):
            far = levels[np.abs(levels - a[p, g]) >= 10]
            a[p, g + 8] = far[np.random.randint(len(far))]
    return np.exp2(a.ravel()).repeat(32)


def f64(x):
    return np.asarray(x).astype(np.float64)


def striped(idx):
    return np.tile(idx.reshape(-1, 16).T, (8, 1)).astype(np.uint16)


def unstriped(offs):
    return offs[:16].T.reshape(-1).astype(np.int64)


def pack_weight(w):
    k, n = w.shape
    w = f64(np.asarray(w, np.float32).astype(ml_dtypes.bfloat16)).reshape(k // 32, 32, n)
    amax = np.abs(w).max(1)
    byte = np.clip(np.where(amax > 0, np.frexp(amax)[1] - 1 + 127 - 7, 1), 1, 254)
    scaled = (w * np.exp2(127.0 - byte)[:, None, :]).reshape(k, n).astype(np.float32)
    words = np.ascontiguousarray(scaled.reshape(k // 512, 128, 4, n).transpose(0, 1, 3, 2)).astype(ml_dtypes.float8_e4m3fn).view(np.uint8)
    return words, np.ascontiguousarray(byte.astype(np.uint8).reshape(k // 512, 16, n))


def unpack_weight(words, scales):
    g, p, n, _ = words.shape
    vals = np.ascontiguousarray(words).view(ml_dtypes.float8_e4m3fn).astype(np.float64) * np.repeat(np.exp2(scales.astype(np.float64) - 127.0), 8, axis=1)[..., None]
    return vals.transpose(0, 1, 3, 2).reshape(g * 512, n)


K, T, S, H, Z, W = 512, 1024, 512, 512, 512, 2048
P = 2 ** 7


def setup_inputs():
    n = np.random.standard_normal
    s = mx_kscale(K)[:, None]
    u = mx_kscale(H)
    packed_xT = pack_weight(n((K, T)) * s)
    packed_eT = pack_weight(n((K, W)) * s)
    return {
        "x_words": packed_xT[0],
        "x_scales": packed_xT[1],
        "w1": (n((K, H)) / np.sqrt(K) / s).astype(np.float32),
        "e_words": packed_eT[0],
        "e_scales": packed_eT[1],
        "w2": (n((K, H)) / np.sqrt(K) / s).astype(np.float32),
        "unit": (np.random.uniform(0.6, 1.4, (H, 1)) * u[:, None]).astype(np.float32),
        "unit2": (np.random.uniform(0.6, 1.4, (H, 1)) / np.sqrt(H) / u[:, None]).astype(np.float32),
        "fare": (np.tile(np.random.uniform(0.1, 0.8, W), (P, 1))).astype(np.float32),
        "offs": striped(np.random.permutation(T)[:S]),
        "dst": striped(np.random.permutation(W)[:Z]),
        "hb": striped(np.random.permutation(S)),
        "tr1": striped(np.random.permutation(Z)),
        "tr2": striped(np.random.permutation(Z)),
    }


def reference(x_words, x_scales, w1, e_words, e_scales, w2, unit, unit2, fare, offs, dst, hb, tr1, tr2):
    xq = unpack_weight(x_words, x_scales)[:, unstriped(offs)]
    y = mxq(f64(w1), 0, "e4m3").T @ xq
    yh = y[:, unstriped(hb)]
    acc_ = np.maximum(y, 0.8 * yh)
    hid = f64(unit) * acc_
    e_dst = unpack_weight(e_words, e_scales)[:, unstriped(dst)]
    ye = mxq(f64(w2), 0, "e4m3").T @ e_dst
    hid2 = f64(unit2) * ye
    sc = mxq(hid, 0, "e4m3").T @ mxq(hid2, 0, "e4m3")
    sa = sc[:, unstriped(tr1)]
    sb = 0.5 * sc[:, unstriped(tr2)]
    cst = np.minimum(sc, sa + sb + f64(fare)[:1][:, unstriped(dst)])
    return np.exp(-1.2 * np.tanh(cst))

from contextlib import ExitStack

import concourse.mybir as mybir

F32 = mybir.dt.float32
BF16 = mybir.dt.bfloat16
I32 = mybir.dt.int32
U32 = mybir.dt.uint32
U16 = mybir.dt.uint16
U8 = mybir.dt.uint8
FP8X4 = mybir.dt.float8_e4m3fn_x4
ALU = mybir.AluOpType
ACT = mybir.ActivationFunctionType

P = 128
PACK = 4
N = 512
HALF = N // 2
SPARE = 16
FLOPS = 3 * 2 * 512 * 512 * 512


def tile_picked_yodtrn_logit_p_kernel(
    tc, x_words, x_scales, w1, e_words, e_scales, w2, unit, unit2, fare, offs, dst, hb, tr1, tr2, out
):
    nc = tc.nc
    x_cols = x_words.shape[2]
    e_cols = e_words.shape[2]

    with ExitStack() as ctx:
        keep = ctx.enter_context(tc.tile_pool(name="keep", bufs=1))
        psum = ctx.enter_context(tc.psum_pool(name="psum", bufs=4))

        def sbuf(name, shape, dtype):
            return keep.tile(shape, dtype, name=name, align_bytes=64)

        def load_list(name, src):
            entries = sbuf(name, list(src.shape), U16)
            nc.sync.dma_start(entries[:], src)
            return entries

        def load_words(name, src, cols):
            table = sbuf(name, [P, cols], I32)
            nc.sync.dma_start(table[:], src[0].rearrange("p n r -> p (n r)").bitcast(I32))
            return table

        def cleared_scale_table(name, cols):
            table = sbuf(name, [P, cols], U8)
            nc.gpsimd.memset(table[:].bitcast(I32), 0)
            return table

        def load_scale_rows(table, src):
            for q in range(4):
                nc.sync.dma_start(
                    table[32 * q : 32 * q + 4, :].bitcast(I32), src[0, 4 * q : 4 * q + 4, :].bitcast(I32)
                )

        def load_weight(name, src, start, width):
            raw = sbuf(name, [P, PACK, width], F32)
            nc.sync.dma_start(raw[:], src.rearrange("(p j) c -> p j c", j=PACK)[:, :, start : start + width])
            return raw

        def load_factor(name, src):
            factor = sbuf(name, [P, PACK], F32)
            nc.sync.dma_start(factor[:], src.rearrange("(p t) o -> p (t o)", t=PACK))
            return factor

        x_scale_table = cleared_scale_table("x_scale_table", x_cols)
        e_scale_table = cleared_scale_table("e_scale_table", e_cols)
        offs_sb = load_list("offs_sb", offs)
        x_word_table = load_words("x_word_table", x_words, x_cols)
        load_scale_rows(x_scale_table, x_scales)
        w1_raw = [load_weight("w1_raw%d" % h, w1, h * HALF, HALF) for h in range(2)]
        unit_sb = load_factor("unit_sb", unit)
        hb_sb = load_list("hb_sb", hb)
        w2_raw = load_weight("w2_raw", w2, 0, N)
        dst_sb = load_list("dst_sb", dst)
        load_scale_rows(e_scale_table, e_scales)
        e_word_table = load_words("e_word_table", e_words, e_cols)
        unit2_sb = load_factor("unit2_sb", unit2)
        tr1_sb = load_list("tr1_sb", tr1)
        tr2_sb = load_list("tr2_sb", tr2)
        fare_table = keep.tile([P, e_cols], F32, name="fare_table", tag="fare", align_bytes=64)
        nc.sync.dma_start(fare_table[:], fare)

        def pick(name, word_table, scale_table, entries, pieces):
            scales = sbuf(name + "_scales", [P, N], U8)
            nc.vector.tensor_copy(scales[:], scale_table[:].indirect(entries[:]))
            words = sbuf(name + "_words", [P, N], U32)
            step = N // pieces
            for a in range(0, N, step):
                part = entries[:, a // 16 : (a + step) // 16]
                nc.vector.tensor_copy(words[:, a : a + step], word_table[:].bitcast(U32).indirect(part))
            return words, scales

        def round_weight(grouped, raw, start, copy):
            cols = slice(start // PACK, (start + raw.shape[2]) // PACK)
            copy(
                grouped[:, :, cols, :].rearrange("p t m j -> p m j t"),
                raw[:].rearrange("p j (m t) -> p m j t", t=PACK),
            )

        def quantize(name, values, pieces):
            width = values.shape[1] // PACK
            words = sbuf(name + "_words", [P, width], U32)
            scales = sbuf(name + "_scales", [P, width], U8)
            step = width // pieces
            for a in range(0, width, step):
                nc.vector.quantize_mx(
                    out=words[:, a : a + step].bitcast(FP8X4),
                    scales=scales[:, a : a + step],
                    in_=values[:, PACK * a : PACK * (a + step)],
                )
            return words, scales

        def product(acc, left, left_cols, right, right_cols):
            nc.tensor.matmul_mx(
                out=acc,
                lhsT=left[0][:, left_cols].bitcast(FP8X4),
                lhsT_scale=left[1][:, left_cols],
                rhs=right[0][:, right_cols].bitcast(FP8X4),
                rhs_scale=right[1][:, right_cols],
                start=True,
                stop=True,
            )

        def block(b):
            return slice(b * P, (b + 1) * P)

        everything = slice(0, N)

        unit_abs = sbuf("unit_abs", [P, PACK], F32)
        nc.scalar.activation(unit_abs[:], unit_sb[:], ACT.Abs)
        unit_sign = sbuf("unit_sign", [P, PACK], F32)
        nc.scalar.activation(unit_sign[:], unit_sb[:], ACT.Sign)
        unit2_signed = keep.tile([P, PACK], F32, name="unit2_signed", tag="hid", align_bytes=64)
        nc.gpsimd.tensor_tensor(unit2_signed[:], unit2_sb[:], unit_sign[:], ALU.mult)

        x_picked = pick("x_picked", x_word_table, x_scale_table, offs_sb, 1)
        w1_grouped = sbuf("w1_grouped", [P, PACK, P, PACK], BF16)
        round_weight(w1_grouped, w1_raw[0], 0, nc.scalar.copy)
        round_weight(w1_grouped, w1_raw[1], HALF, nc.vector.tensor_copy)
        w1_mx = quantize("w1_mx", w1_grouped[:].rearrange("p t m j -> p (t m j)"), 2)

        y_scaled = sbuf("y_scaled", [P, PACK, N], F32)
        for t in range(PACK):
            acc = psum.tile([P, N], F32, name="y_acc", tag="wide")
            product(acc[:], w1_mx, block(t), x_picked, everything)
            nc.scalar.activation(y_scaled[:, t, :], acc[:], ACT.Copy, scale=unit_abs[:, t : t + 1])

        w2_grouped = sbuf("w2_grouped", [P, PACK, P, PACK], BF16)
        round_weight(w2_grouped, w2_raw, 0, nc.vector.tensor_copy)
        w2_mx = quantize("w2_mx", w2_grouped[:].rearrange("p t m j -> p (t m j)"), 1)
        e_picked = pick("e_picked", e_word_table, e_scale_table, dst_sb, 2)

        hub = sbuf("hub", [P, 2, PACK, HALF], F32)
        for h in range(2):
            entries = hb_sb[:, h * HALF // 16 : (h + 1) * HALF // 16]
            for t in range(PACK):
                nc.scalar.activation(hub[:, h, t, :], y_scaled[:, t, :].indirect(entries), ACT.Copy, scale=0.8)

        def larger(name, tag, start, width):
            hid = keep.tile([P, width, PACK], BF16, name=name, tag=tag, align_bytes=64)
            within = start % HALF
            nc.vector.tensor_tensor(
                hid[:].rearrange("p (c i) t -> p c t i", i=4),
                y_scaled[:, :, start : start + width].rearrange("p t (c i) -> p c t i", i=4),
                hub[:, start // HALF, :, within : within + width].rearrange("p t (c i) -> p c t i", i=4),
                ALU.max,
            )
            return hid[:].rearrange("p n t -> p (n t)")

        hid2 = keep.tile([P, N, PACK], BF16, name="hid2", tag="hid2", align_bytes=64)
        for b in range(N // P):
            acc = psum.tile([P, PACK, P], F32, name="ye_acc", tag="ye")
            for t in range(PACK):
                product(acc[:, t, :], w2_mx, block(t), e_picked, block(b))
            nc.vector.tensor_tensor(
                hid2[:, block(b), :],
                acc[:].rearrange("p t n -> p n t"),
                unit2_signed[:].unsqueeze(1).to_broadcast([P, P, PACK]),
                ALU.mult,
            )
        hid_a = larger("hid_a", "hid", 0, P)
        hid2_mx = quantize("hid2_mx", hid2[:].rearrange("p n t -> p (n t)"), 2)
        hid_a_mx = quantize("hid_a_mx", hid_a, 1)
        hid_b_mx = quantize("hid_b_mx", larger("hid_b", "hid2", P, P), 1)
        hid_c_mx = quantize("hid_c_mx", larger("hid_c", "hid", HALF, HALF), 1)
        stationary = [(hid_a_mx, 0), (hid_b_mx, 0), (hid_c_mx, 0), (hid_c_mx, 1)]

        fare_picked = sbuf("fare_picked", [P, N], F32)
        nc.scalar.activation(fare_picked[:], fare_table[:].indirect(dst_sb[:]), ACT.Copy)

        tiles = N // P
        accs, sc, first, second = [], [], [], []
        for m in range(tiles):
            accs.append(psum.tile([P, N], F32, name="sc_acc", tag="wide"))
            product(accs[m][:], stationary[m][0], block(stationary[m][1]), hid2_mx, everything)
            first.append(sbuf("first%d" % m, [P, N], F32))
            second.append(sbuf("second%d" % m, [P, N], F32))

        def bring_out(m):
            sc.append(keep.tile([P, N + SPARE], F32, name="sc", tag="sc%d" % m if m else "fare", align_bytes=64))
            nc.gpsimd.memset(sc[m][:, N:], 0.0)
            nc.scalar.copy(sc[m][:, :N], accs[m][:])
            nc.vector.tensor_tensor(first[m][:], sc[m][:].indirect(tr1_sb[:]), fare_picked[:], ALU.add)

        def second_leg(m):
            nc.scalar.activation(second[m][:], sc[m][:].indirect(tr2_sb[:]), ACT.Copy, scale=0.5)

        def by_transfer(m, cols):
            nc.vector.tensor_tensor(first[m][:, cols], first[m][:, cols], second[m][:, cols], ALU.add)

        def cheaper(m, cols):
            nc.vector.tensor_tensor(first[m][:, cols], first[m][:, cols], accs[m][:, cols], ALU.min)

        def squash(m, cols):
            nc.scalar.activation(second[m][:, cols], first[m][:, cols], ACT.Tanh)

        def finish(m, cols):
            nc.scalar.activation(first[m][:, cols], second[m][:, cols], ACT.Exp, scale=-1.2)
            nc.sync.dma_start(out[block(m), cols], first[m][:, cols])

        last = tiles - 1
        halves = [slice(0, HALF), slice(HALF, N)]
        bring_out(0)
        bring_out(1)
        second_leg(0)
        for m in range(last):
            by_transfer(m, everything)
            second_leg(m + 1)
            cheaper(m, everything)
            if m + 2 < tiles:
                bring_out(m + 2)
            squash(m, everything)
            finish(m, everything)
        for step in (by_transfer, cheaper, squash, finish):
            for cols in halves:
                step(last, cols)
